import numpy as np
import ml_dtypes


def mxq(x, axis, fmt="e4m3"):
    dtype, down = {"e4m3": (ml_dtypes.float8_e4m3fn, 7), "e5m2": (ml_dtypes.float8_e5m2, 14)}[fmt]
    v = np.moveaxis(np.asarray(x, np.float32).astype(ml_dtypes.bfloat16).astype(np.float64), axis, -1)
    blocks = v.reshape(v.shape[:-1] + (-1, 32))
    amax = np.abs(blocks).max(-1, keepdims=True)
    byte = np.maximum(np.where(amax > 0, np.frexp(amax)[1] - 1 + 127, 0) - down, 1)
    scale = np.exp2(byte - 127.0)
    codes = (blocks / scale).astype(np.float32).astype(dtype).astype(np.float64)
    return np.moveaxis((codes * scale).reshape(v.shape), -1, axis)


WIDE = False


def mx_kscale(k):
    if not WIDE:
        return np.ones(k)
    levels = np.array([10, -10, 5, -5, 0])
    if k % 512:
        return np.exp2(np.random.permutation(np.resize(levels, k // 32))).repeat(32)
    a = np.empty((k // 512, 16))
    for p in range(k // 512):
        a[p, :8] = np.random.permutation(np.resize(levels, 8))
        for g in range(8):
            far = levels[np.abs(levels - a[p, g]) >= 10]
            a[p, g + 8] = far[np.random.randint(len(far))]
    return np.exp2(a.ravel()).repeat(32)


def f64(x):
    return np.asarray(x).astype(np.float64)


def striped(idx):
    return np.tile(idx.reshape(-1, 16).T, (8, 1)).astype(np.uint16)


def unstriped(offs):
    return offs[:16].T.reshape(-1).astype(np.int64)


def sigmoid(v):
    return 1.0 / (1.0 + np.exp(-np.maximum(v, -700.0)))


K, T, D, S, V, N = 1536, 1024, 2, 512, 256, 128


def setup_inputs():
    n = np.random.standard_normal
    s = mx_kscale(K)[:, None]
    return {
        "xT": (n((K, T)) * s).astype(np.float32),
        "w": (n((D, K, N)) / np.sqrt(K) / s[None]).astype(np.float32),
        "b": (0.3 * n((N, 1))).astype(np.float32),
        "offs": striped(np.random.permutation(T)[:S]),
    }


def reference(xT, w, b, offs):
    idx = unstriped(offs)
    xq = mxq(f64(xT)[:, idx], 0, "e4m3")
    wq = mxq(f64(w), 1, "e4m3")
    y0 = wq[0].T @ xq[:, :V]
    y1 = wq[1].T @ xq[:, V:]
    return y0 * sigmoid(y1 + f64(b))

@@ -1,0 +1,144 @@
+from contextlib import ExitStack
+
+import concourse.mybir as mybir
+
+K, T, D, S, V, N = 1536, 1024, 2, 512, 256, 128
+FLOPS = 2 * K * N * S
+
+F32 = mybir.dt.float32
+BF16 = mybir.dt.bfloat16
+U32 = mybir.dt.uint32
+U16 = mybir.dt.uint16
+U8 = mybir.dt.uint8
+FP8X4 = mybir.dt.float8_e4m3fn_x4
+SIGMOID = mybir.ActivationFunctionType.Sigmoid
+MULT = mybir.AluOpType.mult
+
+P = 128
+PASSES = 3
+
+
+def tile_picked_pair_lin_gate_sub_e_kernel(tc, xT, w, b, offs, out):
+    nc = tc.nc
+    with ExitStack() as ctx:
+        held = ctx.enter_context(tc.tile_pool(name="held", bufs=1))
+        psum = ctx.enter_context(tc.psum_pool(name="psum", bufs=1))
+
+        offsets = held.tile([P, S // 16], U16, name="offsets")
+        bias = held.tile([P, 1], F32, name="bias")
+        warm = held.tile([P, 1], F32, name="warm")
+        x_raw, pairs, x_grouped, x_codes, x_scales = {}, {}, {}, {}, {}
+        w_raw, w_grouped, w_codes, w_scales = {}, {}, {}, {}
+        for a in range(PASSES):
+            for u in range(2):
+                x_raw[a, u] = held.tile([P, 2, T], F32, name=f"x_raw{a}{u}")
+                pairs[a, u] = held.tile([P, 2 * T], BF16, name=f"pairs{a}{u}", align_bytes=64)
+            x_grouped[a] = held.tile([P, 4 * S], BF16, name=f"x_grouped{a}", align_bytes=64)
+            x_codes[a] = held.tile([P, S], U32, name=f"x_codes{a}", align_bytes=64)
+            x_scales[a] = held.tile([P, S], U8, name=f"x_scales{a}", align_bytes=64)
+            for d in range(D):
+                w_raw[a, d] = held.tile([P, 4, N], F32, name=f"w_raw{a}{d}")
+                w_grouped[a, d] = held.tile([P, 4 * N], BF16, name=f"w_grouped{a}{d}", align_bytes=64)
+                w_codes[a, d] = held.tile([P, N], U32, name=f"w_codes{a}{d}", align_bytes=64)
+                w_scales[a, d] = held.tile([P, N], U8, name=f"w_scales{a}{d}", align_bytes=64)
+
+        y = [psum.tile([P, V], F32, name=f"y{d}") for d in range(D)]
+
+        def load_x(a, u):
+            rows = xT[512 * a : 512 * (a + 1), :].rearrange("(p j) t -> p j t", j=4)
+            nc.sync.dma_start(out=x_raw[a, u][:], in_=rows[:, 2 * u : 2 * u + 2, :])
+
+        def load_w(a, d):
+            rows = w[d, 512 * a : 512 * (a + 1), :].rearrange("(p j) m -> p j m", j=4)
+            nc.sync.dma_start(out=w_raw[a, d][:], in_=rows)
+
+        def cast_x(a, u, cut):
+            dst = pairs[a, u][:].rearrange("p (t e) -> p t e", e=2)
+            raw = x_raw[a, u][:].rearrange("p e t -> p t e")
+            if cut < T:
+                nc.scalar.copy(out=dst[:, cut:, :], in_=raw[:, cut:, :])
+            if cut > 0:
+                nc.vector.tensor_copy(out=dst[:, :cut, :], in_=raw[:, :cut, :])
+
+        def gather(a, u):
+            words = x_grouped[a][:].bitcast(U32)
+            nc.vector.tensor_copy(out=words[:, u::2], in_=pairs[a, u][:].bitcast(U32).indirect(offsets[:]))
+
+        def quantize_x(a):
+            nc.vector.quantize_mx(out=x_codes[a][:].bitcast(FP8X4), scales=x_scales[a][:], in_=x_grouped[a][:])
+
+        def cast_w(a, d, cut):
+            dst = w_grouped[a, d][:].rearrange("p (m j) -> p m j", j=4)
+            raw = w_raw[a, d][:].rearrange("p j m -> p m j")
+            if cut < N:
+                nc.scalar.copy(out=dst[:, cut:, :], in_=raw[:, cut:, :])
+            if cut > 0:
+                nc.vector.tensor_copy(out=dst[:, :cut, :], in_=raw[:, :cut, :])
+
+        def quantize_w(a, d):
+            nc.vector.quantize_mx(out=w_codes[a, d][:].bitcast(FP8X4), scales=w_scales[a, d][:], in_=w_grouped[a, d][:])
+
+        def multiply(a, d):
+            cols = slice(d * V, (d + 1) * V)
+            nc.tensor.matmul_mx(
+                out=y[d][:],
+                lhsT=w_codes[a, d][:].bitcast(FP8X4),
+                lhsT_scale=w_scales[a, d][:],
+                rhs=x_codes[a][:, cols].bitcast(FP8X4),
+                rhs_scale=x_scales[a][:, cols],
+                start=(a == 0),
+                stop=(a == PASSES - 1),
+            )
+
+        for d in (1, 0):
+            load_w(0, d)
+        load_x(0, 0)
+        nc.sync.dma_start(offsets[:], offs)
+        nc.scalar.dma_start(out=bias[:], in_=b)
+        nc.vector.memset(warm[:], 0.0)
+        nc.scalar.activation(out=warm[:], in_=warm[:], func=SIGMOID)
+        for a, u in ((0, 1), (1, 0), (1, 1), (2, 0), (2, 1)):
+            load_x(a, u)
+        for a in (1, 2):
+            for d in (1, 0):
+                load_w(a, d)
+
+        for d in (1, 0):
+            cast_w(0, d, 64)
+        for d in (1, 0):
+            quantize_w(0, d)
+        cast_x(0, 0, 256)
+        cast_x(0, 1, 256)
+        gather(0, 0)
+        cast_x(1, 0, 256)
+        gather(0, 1)
+        cast_x(1, 1, 256)
+        gather(1, 0)
+        quantize_x(0)
+        for d in (1, 0):
+            multiply(0, d)
+        cast_x(2, 0, 384)
+        gather(1, 1)
+        cast_x(2, 1, 448)
+        gather(2, 0)
+        quantize_x(1)
+        cast_w(1, 1, 0)
+        gather(2, 1)
+        quantize_w(1, 1)
+        cast_w(1, 0, 0)
+        quantize_w(1, 0)
+        for d in (1, 0):
+            multiply(1, d)
+        quantize_x(2)
+        cast_w(2, 1, 0)
+        quantize_w(2, 1)
+        cast_w(2, 0, 128)
+        multiply(2, 1)
+        quantize_w(2, 0)
+        multiply(2, 0)
+
+        gate = held.tile([P, V], F32, name="gate")
+        result = held.tile([P, V], F32, name="result")
+        nc.scalar.activation(out=gate[:], in_=y[1][:], func=SIGMOID, bias=bias[:])
+        nc.vector.tensor_tensor(out=result[:], in0=y[0][:], in1=gate[:], op=MULT)
+        nc.sync.dma_start(out=out, in_=result[:])

@@ -13,6 +13,8 @@ U8 = mybir.dt.uint8
 FP8X4 = mybir.dt.float8_e4m3fn_x4
 SIGMOID = mybir.ActivationFunctionType.Sigmoid
 MULT = mybir.AluOpType.mult
+ADD = mybir.AluOpType.add
+COPY = (1, 1, 1)
 
 P = 128
 PASSES = 3
@@ -27,20 +29,20 @@ def tile_picked_pair_lin_gate_sub_e_kernel(tc, xT, w, b, offs, out):
         offsets = held.tile([P, S // 16], U16, name="offsets")
         bias = held.tile([P, 1], F32, name="bias")
         warm = held.tile([P, 1], F32, name="warm")
-        x_raw, pairs, x_grouped, x_codes, x_scales = {}, {}, {}, {}, {}
+        x_raw, pairs, gathered, x_grouped, x_codes, x_scales = {}, {}, {}, {}, {}, {}
         w_raw, w_grouped, w_codes, w_scales = {}, {}, {}, {}
         for a in range(PASSES):
             for u in range(2):
                 x_raw[a, u] = held.tile([P, 2, T], F32, name=f"x_raw{a}{u}")
                 pairs[a, u] = held.tile([P, 2 * T], BF16, name=f"pairs{a}{u}", align_bytes=64)
+            gathered[a] = held.tile([P, 4 * S], BF16, name=f"gathered{a}", align_bytes=64)
             x_grouped[a] = held.tile([P, 4 * S], BF16, name=f"x_grouped{a}", align_bytes=64)
             x_codes[a] = held.tile([P, S], U32, name=f"x_codes{a}", align_bytes=64)
             x_scales[a] = held.tile([P, S], U8, name=f"x_scales{a}", align_bytes=64)
-            for d in range(D):
-                w_raw[a, d] = held.tile([P, 4, N], F32, name=f"w_raw{a}{d}")
-                w_grouped[a, d] = held.tile([P, 4 * N], BF16, name=f"w_grouped{a}{d}", align_bytes=64)
-                w_codes[a, d] = held.tile([P, N], U32, name=f"w_codes{a}{d}", align_bytes=64)
-                w_scales[a, d] = held.tile([P, N], U8, name=f"w_scales{a}{d}", align_bytes=64)
+            w_raw[a] = held.tile([P, D, 4, N], F32, name=f"w_raw{a}")
+            w_grouped[a] = held.tile([P, D * 4 * N], BF16, name=f"w_grouped{a}", align_bytes=64)
+            w_codes[a] = held.tile([P, D * N], U32, name=f"w_codes{a}", align_bytes=64)
+            w_scales[a] = held.tile([P, D * N], U8, name=f"w_scales{a}", align_bytes=64)
 
         y = [psum.tile([P, V], F32, name=f"y{d}") for d in range(D)]
 
@@ -48,93 +50,112 @@ def tile_picked_pair_lin_gate_sub_e_kernel(tc, xT, w, b, offs, out):
             rows = xT[512 * a : 512 * (a + 1), :].rearrange("(p j) t -> p j t", j=4)
             nc.sync.dma_start(out=x_raw[a, u][:], in_=rows[:, 2 * u : 2 * u + 2, :])
 
-        def load_w(a, d):
-            rows = w[d, 512 * a : 512 * (a + 1), :].rearrange("(p j) m -> p j m", j=4)
-            nc.sync.dma_start(out=w_raw[a, d][:], in_=rows)
+        def load_w(a, d, n):
+            if n == 1:
+                rows = w[d, 512 * a : 512 * (a + 1), :].rearrange("(p j) m -> p j m", j=4)
+                nc.sync.dma_start(out=w_raw[a][:, d, :, :], in_=rows)
+            else:
+                rows = w[:, 512 * a : 512 * (a + 1), :].rearrange("d (p j) m -> p d (j m)", j=4)
+                nc.sync.dma_start(out=w_raw[a][:].rearrange("p d j m -> p d (j m)"), in_=rows)
 
-        def cast_x(a, u, cut):
+        def split_copy(dst, src, at, v, g, n):
+            if v > 0:
+                nc.vector.tensor_copy(out=at(dst, 0, v), in_=at(src, 0, v))
+            if v + g < n:
+                nc.scalar.copy(out=at(dst, v, n - g), in_=at(src, v, n - g))
+            if g > 0:
+                nc.gpsimd.tensor_scalar(out=at(dst, n - g, n), in0=at(src, n - g, n), scalar1=1.0, scalar2=0.0, op0=MULT, op1=ADD)
+
+        def cast_x(a, u, v, g):
             dst = pairs[a, u][:].rearrange("p (t e) -> p t e", e=2)
-            raw = x_raw[a, u][:].rearrange("p e t -> p t e")
-            if cut < T:
-                nc.scalar.copy(out=dst[:, cut:, :], in_=raw[:, cut:, :])
-            if cut > 0:
-                nc.vector.tensor_copy(out=dst[:, :cut, :], in_=raw[:, :cut, :])
+            src = x_raw[a, u][:].rearrange("p e t -> p t e")
+            split_copy(dst, src, lambda ap, lo, hi: ap[:, lo:hi, :], v, g, T)
 
         def gather(a, u):
-            words = x_grouped[a][:].bitcast(U32)
-            nc.vector.tensor_copy(out=words[:, u::2], in_=pairs[a, u][:].bitcast(U32).indirect(offsets[:]))
+            if COPY[a]:
+                words = gathered[a][:].bitcast(U32)[:, u * S : (u + 1) * S]
+            else:
+                words = x_grouped[a][:].bitcast(U32)[:, u::2]
+            nc.vector.tensor_copy(out=words, in_=pairs[a, u][:].bitcast(U32).indirect(offsets[:]))
 
-        def quantize_x(a):
-            nc.vector.quantize_mx(out=x_codes[a][:].bitcast(FP8X4), scales=x_scales[a][:], in_=x_grouped[a][:])
+        def interleave(a):
+            nc.vector.tensor_copy(
+                out=x_grouped[a][:].rearrange("p (s u e) -> p s u e", u=2, e=2),
+                in_=gathered[a][:].rearrange("p (u s e) -> p s u e", u=2, e=2),
+            )
 
-        def cast_w(a, d, cut):
-            dst = w_grouped[a, d][:].rearrange("p (m j) -> p m j", j=4)
-            raw = w_raw[a, d][:].rearrange("p j m -> p m j")
-            if cut < N:
-                nc.scalar.copy(out=dst[:, cut:, :], in_=raw[:, cut:, :])
-            if cut > 0:
-                nc.vector.tensor_copy(out=dst[:, :cut, :], in_=raw[:, :cut, :])
+        def quantize_x(a, lo, hi):
+            nc.vector.quantize_mx(out=x_codes[a][:, lo:hi].bitcast(FP8X4), scales=x_scales[a][:, lo:hi], in_=x_grouped[a][:, 4 * lo : 4 * hi])
 
-        def quantize_w(a, d):
-            nc.vector.quantize_mx(out=w_codes[a, d][:].bitcast(FP8X4), scales=w_scales[a, d][:], in_=w_grouped[a, d][:])
+        def cast_w(a, d, n, v, g):
+            dst = w_grouped[a][:].rearrange("p (d m j) -> p d m j", d=D, j=4)
+            src = w_raw[a][:].rearrange("p d j m -> p d m j")
+            if n == 1:
+                split_copy(dst[:, d], src[:, d], lambda ap, lo, hi: ap[:, lo:hi, :], v, g, N)
+            else:
+                split_copy(dst, src, lambda ap, lo, hi: ap[:, :, lo:hi, :], v, g, N)
+
+        def quantize_w(a, d, n):
+            lo, hi = d * N, (d + n) * N
+            nc.vector.quantize_mx(out=w_codes[a][:, lo:hi].bitcast(FP8X4), scales=w_scales[a][:, lo:hi], in_=w_grouped[a][:, 4 * lo : 4 * hi])
 
         def multiply(a, d):
             cols = slice(d * V, (d + 1) * V)
             nc.tensor.matmul_mx(
                 out=y[d][:],
-                lhsT=w_codes[a, d][:].bitcast(FP8X4),
-                lhsT_scale=w_scales[a, d][:],
+                lhsT=w_codes[a][:, d * N : (d + 1) * N].bitcast(FP8X4),
+                lhsT_scale=w_scales[a][:, d * N : (d + 1) * N],
                 rhs=x_codes[a][:, cols].bitcast(FP8X4),
                 rhs_scale=x_scales[a][:, cols],
                 start=(a == 0),
                 stop=(a == PASSES - 1),
             )
 
-        for d in (1, 0):
-            load_w(0, d)
         load_x(0, 0)
-        nc.sync.dma_start(offsets[:], offs)
         nc.scalar.dma_start(out=bias[:], in_=b)
         nc.vector.memset(warm[:], 0.0)
         nc.scalar.activation(out=warm[:], in_=warm[:], func=SIGMOID)
-        for a, u in ((0, 1), (1, 0), (1, 1), (2, 0), (2, 1)):
-            load_x(a, u)
-        for a in (1, 2):
-            for d in (1, 0):
-                load_w(a, d)
-
-        for d in (1, 0):
-            cast_w(0, d, 64)
-        for d in (1, 0):
-            quantize_w(0, d)
-        cast_x(0, 0, 256)
-        cast_x(0, 1, 256)
+        nc.sync.dma_start(offsets[:], offs)
+        load_x(0, 1)
+        load_x(1, 0)
+        load_x(1, 1)
+        load_x(2, 0)
+        load_x(2, 1)
+        load_w(0, 0, 2)
+        load_w(1, 0, 2)
+        load_w(2, 1, 1)
+        load_w(2, 0, 1)
+        cast_x(0, 0, 544, 0)
+        cast_x(0, 1, 448, 0)
         gather(0, 0)
-        cast_x(1, 0, 256)
+        cast_x(1, 0, 256, 0)
         gather(0, 1)
-        cast_x(1, 1, 256)
+        interleave(0)
         gather(1, 0)
-        quantize_x(0)
-        for d in (1, 0):
-            multiply(0, d)
-        cast_x(2, 0, 384)
+        cast_x(1, 1, 320, 0)
+        quantize_x(0, 0, S)
         gather(1, 1)
-        cast_x(2, 1, 448)
+        cast_x(2, 0, 192, 0)
+        interleave(1)
         gather(2, 0)
-        quantize_x(1)
-        cast_w(1, 1, 0)
+        cast_x(2, 1, 192, 0)
+        cast_w(0, 0, 2, 64, 0)
+        quantize_x(1, 0, S)
+        cast_w(1, 0, 2, 16, 0)
         gather(2, 1)
-        quantize_w(1, 1)
-        cast_w(1, 0, 0)
-        quantize_w(1, 0)
-        for d in (1, 0):
-            multiply(1, d)
-        quantize_x(2)
-        cast_w(2, 1, 0)
-        quantize_w(2, 1)
-        cast_w(2, 0, 128)
+        quantize_w(0, 0, 2)
+        multiply(0, 1)
+        multiply(0, 0)
+        interleave(2)
+        quantize_w(1, 0, 2)
+        multiply(1, 1)
+        multiply(1, 0)
+        quantize_x(2, 0, S)
+        cast_w(2, 1, 1, 0, 0)
+        quantize_w(2, 1, 1)
         multiply(2, 1)
-        quantize_w(2, 0)
+        cast_w(2, 0, 1, 32, 0)
+        quantize_w(2, 0, 1)
         multiply(2, 0)
 
         gate = held.tile([P, V], F32, name="gate")

from contextlib import ExitStack

import concourse.mybir as mybir

K, T, D, S, V, N = 1536, 1024, 2, 512, 256, 128
FLOPS = 2 * K * N * S

F32 = mybir.dt.float32
BF16 = mybir.dt.bfloat16
U32 = mybir.dt.uint32
U16 = mybir.dt.uint16
U8 = mybir.dt.uint8
FP8X4 = mybir.dt.float8_e4m3fn_x4
SIGMOID = mybir.ActivationFunctionType.Sigmoid
MULT = mybir.AluOpType.mult
ADD = mybir.AluOpType.add
COPY = (1, 1, 1)

P = 128
PASSES = 3


def tile_picked_pair_lin_gate_sub_e_kernel(tc, xT, w, b, offs, out):
    nc = tc.nc
    with ExitStack() as ctx:
        held = ctx.enter_context(tc.tile_pool(name="held", bufs=1))
        psum = ctx.enter_context(tc.psum_pool(name="psum", bufs=1))

        offsets = held.tile([P, S // 16], U16, name="offsets")
        bias = held.tile([P, 1], F32, name="bias")
        warm = held.tile([P, 1], F32, name="warm")
        x_raw, pairs, gathered, x_grouped, x_codes, x_scales = {}, {}, {}, {}, {}, {}
        w_raw, w_grouped, w_codes, w_scales = {}, {}, {}, {}
        for a in range(PASSES):
            for u in range(2):
                x_raw[a, u] = held.tile([P, 2, T], F32, name=f"x_raw{a}{u}")
                pairs[a, u] = held.tile([P, 2 * T], BF16, name=f"pairs{a}{u}", align_bytes=64)
            gathered[a] = held.tile([P, 4 * S], BF16, name=f"gathered{a}", align_bytes=64)
            x_grouped[a] = held.tile([P, 4 * S], BF16, name=f"x_grouped{a}", align_bytes=64)
            x_codes[a] = held.tile([P, S], U32, name=f"x_codes{a}", align_bytes=64)
            x_scales[a] = held.tile([P, S], U8, name=f"x_scales{a}", align_bytes=64)
            w_raw[a] = held.tile([P, D, 4, N], F32, name=f"w_raw{a}")
            w_grouped[a] = held.tile([P, D * 4 * N], BF16, name=f"w_grouped{a}", align_bytes=64)
            w_codes[a] = held.tile([P, D * N], U32, name=f"w_codes{a}", align_bytes=64)
            w_scales[a] = held.tile([P, D * N], U8, name=f"w_scales{a}", align_bytes=64)

        y = [psum.tile([P, V], F32, name=f"y{d}") for d in range(D)]

        def load_x(a, u):
            rows = xT[512 * a : 512 * (a + 1), :].rearrange("(p j) t -> p j t", j=4)
            nc.sync.dma_start(out=x_raw[a, u][:], in_=rows[:, 2 * u : 2 * u + 2, :])

        def load_w(a, d, n):
            if n == 1:
                rows = w[d, 512 * a : 512 * (a + 1), :].rearrange("(p j) m -> p j m", j=4)
                nc.sync.dma_start(out=w_raw[a][:, d, :, :], in_=rows)
            else:
                rows = w[:, 512 * a : 512 * (a + 1), :].rearrange("d (p j) m -> p d (j m)", j=4)
                nc.sync.dma_start(out=w_raw[a][:].rearrange("p d j m -> p d (j m)"), in_=rows)

        def split_copy(dst, src, at, v, g, n):
            if v > 0:
                nc.vector.tensor_copy(out=at(dst, 0, v), in_=at(src, 0, v))
            if v + g < n:
                nc.scalar.copy(out=at(dst, v, n - g), in_=at(src, v, n - g))
            if g > 0:
                nc.gpsimd.tensor_scalar(out=at(dst, n - g, n), in0=at(src, n - g, n), scalar1=1.0, scalar2=0.0, op0=MULT, op1=ADD)

        def cast_x(a, u, v, g):
            dst = pairs[a, u][:].rearrange("p (t e) -> p t e", e=2)
            src = x_raw[a, u][:].rearrange("p e t -> p t e")
            split_copy(dst, src, lambda ap, lo, hi: ap[:, lo:hi, :], v, g, T)

        def gather(a, u):
            if COPY[a]:
                words = gathered[a][:].bitcast(U32)[:, u * S : (u + 1) * S]
            else:
                words = x_grouped[a][:].bitcast(U32)[:, u::2]
            nc.vector.tensor_copy(out=words, in_=pairs[a, u][:].bitcast(U32).indirect(offsets[:]))

        def interleave(a):
            nc.vector.tensor_copy(
                out=x_grouped[a][:].rearrange("p (s u e) -> p s u e", u=2, e=2),
                in_=gathered[a][:].rearrange("p (u s e) -> p s u e", u=2, e=2),
            )

        def quantize_x(a, lo, hi):
            nc.vector.quantize_mx(out=x_codes[a][:, lo:hi].bitcast(FP8X4), scales=x_scales[a][:, lo:hi], in_=x_grouped[a][:, 4 * lo : 4 * hi])

        def cast_w(a, d, n, v, g):
            dst = w_grouped[a][:].rearrange("p (d m j) -> p d m j", d=D, j=4)
            src = w_raw[a][:].rearrange("p d j m -> p d m j")
            if n == 1:
                split_copy(dst[:, d], src[:, d], lambda ap, lo, hi: ap[:, lo:hi, :], v, g, N)
            else:
                split_copy(dst, src, lambda ap, lo, hi: ap[:, :, lo:hi, :], v, g, N)

        def quantize_w(a, d, n):
            lo, hi = d * N, (d + n) * N
            nc.vector.quantize_mx(out=w_codes[a][:, lo:hi].bitcast(FP8X4), scales=w_scales[a][:, lo:hi], in_=w_grouped[a][:, 4 * lo : 4 * hi])

        def multiply(a, d):
            cols = slice(d * V, (d + 1) * V)
            nc.tensor.matmul_mx(
                out=y[d][:],
                lhsT=w_codes[a][:, d * N : (d + 1) * N].bitcast(FP8X4),
                lhsT_scale=w_scales[a][:, d * N : (d + 1) * N],
                rhs=x_codes[a][:, cols].bitcast(FP8X4),
                rhs_scale=x_scales[a][:, cols],
                start=(a == 0),
                stop=(a == PASSES - 1),
            )

        load_x(0, 0)
        nc.scalar.dma_start(out=bias[:], in_=b)
        nc.vector.memset(warm[:], 0.0)
        nc.scalar.activation(out=warm[:], in_=warm[:], func=SIGMOID)
        nc.sync.dma_start(offsets[:], offs)
        load_x(0, 1)
        load_x(1, 0)
        load_x(1, 1)
        load_x(2, 0)
        load_x(2, 1)
        load_w(0, 0, 2)
        load_w(1, 0, 2)
        load_w(2, 1, 1)
        load_w(2, 0, 1)
        cast_x(0, 0, 544, 0)
        cast_x(0, 1, 448, 0)
        gather(0, 0)
        cast_x(1, 0, 256, 0)
        gather(0, 1)
        interleave(0)
        gather(1, 0)
        cast_x(1, 1, 320, 0)
        quantize_x(0, 0, S)
        gather(1, 1)
        cast_x(2, 0, 192, 0)
        interleave(1)
        gather(2, 0)
        cast_x(2, 1, 192, 0)
        cast_w(0, 0, 2, 64, 0)
        quantize_x(1, 0, S)
        cast_w(1, 0, 2, 16, 0)
        gather(2, 1)
        quantize_w(0, 0, 2)
        multiply(0, 1)
        multiply(0, 0)
        interleave(2)
        quantize_w(1, 0, 2)
        multiply(1, 1)
        multiply(1, 0)
        quantize_x(2, 0, S)
        cast_w(2, 1, 1, 0, 0)
        quantize_w(2, 1, 1)
        multiply(2, 1)
        cast_w(2, 0, 1, 32, 0)
        quantize_w(2, 0, 1)
        multiply(2, 0)

        gate = held.tile([P, V], F32, name="gate")
        result = held.tile([P, V], F32, name="result")
        nc.scalar.activation(out=gate[:], in_=y[1][:], func=SIGMOID, bias=bias[:])
        nc.vector.tensor_tensor(out=result[:], in0=y[0][:], in1=gate[:], op=MULT)
        nc.sync.dma_start(out=out, in_=result[:])
